import numpy as np
CORES = [0,8,16,24,32,40,48,56,128,136,144,152,160,168,176,184,256,264,272,280,288,296,304,312,384,392,400,408,416,424,432,440]
N = 32
T = 16
ROUTE = [[[14],[17],[11],[20],[30],[4],[19],[3],[27],[17],[15],[27],[27],[18],[4],[7]],[[15],[20],[27],[19],[24],[27],[27],[27],[7],[27],[27],[0],[27],[27],[27],[27]],[[29],[22],[29],[19],[0],[24],[23],[27],[0],[28],[10],[30],[27],[27],[18],[27]],[[26],[27],[30],[25],[20],[27],[20],[18],[11],[22],[27],[21],[23],[2],[0],[27]],[[27],[27],[7],[27],[27],[4],[27],[0],[23],[27],[26],[27],[27],[29],[27],[27]],[[14],[21],[31],[1],[1],[31],[21],[8],[6],[31],[17],[27],[27],[27],[27],[27]],[[8],[27],[29],[15],[27],[27],[27],[27],[15],[0],[24],[17],[27],[27],[27],[22]],[[27],[12],[24],[24],[27],[27],[10],[24],[4],[31],[27],[27],[27],[18],[27],[19]],[[15],[24],[28],[6],[28],[27],[27],[27],[27],[30],[27],[27],[27],[26],[5],[25]],[[28],[6],[28],[19],[27],[27],[27],[15],[0],[30],[0],[19],[12],[2],[15],[27]],[[23],[7],[27],[15],[17],[21],[16],[18],[11],[13],[27],[3],[20],[6],[22],[22]],[[27],[27],[27],[5],[27],[5],[21],[24],[19],[27],[27],[23],[18],[27],[0],[4]],[[20],[27],[27],[8],[10],[18],[27],[12],[31],[0],[12],[27],[17],[20],[22],[27]],[[27],[5],[27],[27],[27],[27],[27],[7],[12],[27],[23],[27],[5],[9],[31],[20]],[[22],[9],[27],[27],[27],[15],[8],[27],[27],[29],[23],[27],[0],[27],[9],[12]],[[6],[23],[3],[6],[27],[21],[27],[22],[27],[27],[10],[27],[19],[1],[11],[27]],[[28],[31],[12],[27],[23],[11],[21],[20],[7],[23],[13],[19],[25],[14],[27],[5]],[[10],[17],[18],[14],[1],[25],[22],[11],[23],[27],[27],[8],[4],[11],[20],[27]],[[31],[21],[8],[27],[8],[10],[27],[1],[27],[8],[22],[30],[27],[27],[7],[5]],[[27],[6],[11],[2],[29],[3],[27],[8],[25],[10],[18],[29],[27],[26],[23],[25]],[[4],[8],[12],[23],[27],[24],[27],[27],[21],[27],[23],[0],[27],[16],[27],[31]],[[27],[3],[7],[12],[21],[26],[27],[19],[25],[10],[27],[3],[8],[27],[24],[9]],[[31],[2],[9],[22],[17],[27],[27],[11],[26],[27],[31],[12],[27],[14],[18],[27]],[[27],[5],[15],[27],[27],[6],[17],[27],[30],[27],[12],[15],[23],[27],[15],[19]],[[4],[25],[4],[10],[27],[11],[3],[7],[6],[29],[2],[14],[1],[27],[21],[15]],[[27],[10],[27],[12],[15],[5],[2],[1],[10],[14],[12],[27],[27],[31],[18],[2]],[[25],[25],[13],[19],[20],[27],[19],[9],[13],[7],[21],[24],[1],[27],[6],[27]],[[22],[13],[27],[19],[10],[27],[26],[30],[6],[25],[23],[20],[29],[6],[25],[27]],[[17],[5],[27],[0],[31],[6],[27],[28],[27],[10],[18],[9],[27],[27],[27],[19]],[[4],[27],[10],[21],[0],[23],[22],[27],[16],[27],[27],[0],[28],[11],[13],[21]],[[14],[17],[12],[12],[29],[21],[27],[21],[27],[27],[27],[11],[9],[30],[19],[30]],[[14],[27],[0],[27],[19],[27],[29],[3],[25],[1],[22],[3],[7],[27],[27],[27]]]
CAP = 12
YW = 12
def setup_inputs(rng):
    return {"x": rng.standard_normal((N, 128, T), dtype=np.float32)}
def reference(x):
    y = np.full((N, 128, YW), np.nan, x.dtype)
    fill = [0] * N
    for r in range(N):
        for t in range(T):
            for e in ROUTE[r][t]:
                if fill[e] < CAP:
                    y[e][:, fill[e]] = x[r][:, t]
                fill[e] += 1
    return {"y": y}

@@ -1,0 +1,269 @@
+import concourse.bass as bass
+
+SCRATCH = {
+    "xs": ("sbuf", [128, 16], "float32"),
+    "land": ("sbuf", [128, 12], "float32"),
+}
+SEMAPHORES = ["loaded", "stored", "xin", "arrived", "sent"]
+
+ISSUE = 20
+HON = 40
+HOFF = 60
+ORDER = 0.5
+LANE = 16
+RELAY_ON_CABLED_CHIP = True
+
+PLAN = {}
+
+
+def pow2ceil(n):
+    p = 1
+    while p < n:
+        p *= 2
+    return p
+
+
+def popcount(m):
+    n = 0
+    while m:
+        n += m & 1
+        m >>= 1
+    return n
+
+
+def engine_masks(n, base):
+    each = 8 // pow2ceil(n)
+    sizes = [each] * n
+    spare = 8 - each * n
+    for i in range(n):
+        if spare >= each:
+            sizes[i] += each
+            spare -= each
+    masks, at = [], base
+    for s in sizes:
+        masks.append(((1 << s) - 1) << at)
+        at += s
+    return masks
+
+
+def by_width(ws):
+    out = {}
+    for w in ws:
+        out.setdefault(w[1], []).append(w)
+    return [out[k] for k in sorted(out)]
+
+
+def group_time(ws, start, own):
+    end = start
+    i = 0
+    for cl in by_width(ws):
+        off = [w for w in cl if w[2] != own]
+        n = max(len(off), 1)
+        while n > 0:
+            end = max(end, start + i * ISSUE) + LANE * pow2ceil(min(n, 8))
+            n -= 8
+            i += 1
+    return end
+
+
+def chunks(ws, m):
+    ws = sorted(ws, key=lambda w: (w[1], w[0]))
+    return [ws[i:i + m] for i in range(0, len(ws), m)]
+
+
+def pack(cross, plain, m):
+    gc, gp = chunks(cross, m), chunks(plain, m)
+    if gc and gp and len(gc[-1]) + len(gp[-1]) <= m:
+        gc[-1] = gc[-1] + gp.pop()
+    return gc, gp
+
+
+def arrival(p, n):
+    return LANE * (ORDER * (p + 1) + (1.0 - ORDER) * n)
+
+
+def plan_source(r, A, B, S, C, D):
+    best = None
+    A = sorted(A, key=lambda w: (w[1], w[0]))
+    for md in (1, 2, 4, 8):
+        rc, rp = pack(D, C, md)
+        if len(rc) > 4 or len(rc) + len(rp) > 8:
+            continue
+        rel = [(True, g) for g in rc] + [(False, g) for g in rp]
+        rel.sort(key=lambda e: -group_time(e[1], 0, r))
+        for mo in (1, 2, 4, 8):
+            for d in range(len(A) + 1):
+                direct = A[:d]
+                gc, gp = pack(B, A[d:], mo)
+                if S and not gc and not gp:
+                    gp = [[]]
+                if len(gc) > 4 or len(gc) + len(gp) > 7:
+                    continue
+                on = [(True, g) for g in gc] + [(False, g) for g in gp]
+                on.sort(key=lambda e: -group_time(e[1], 0, r))
+                if S:
+                    on[-1] = (on[-1][0], on[-1][1] + S)
+                for nlow in range(len(on) + 1):
+                    nl, nu = len(rel) + nlow, len(on) - nlow
+                    slots = [(arrival(p, nu), 1, p) for p in range(nu)]
+                    slots += [(arrival(p, nl), 0, p) for p in range(len(rel), nl)]
+                    slots.sort()
+                    f = 0
+                    for p, e in enumerate(rel):
+                        f = max(f, group_time(e[1], arrival(p, nl) + HOFF, r))
+                    for sl, e in zip(slots, on):
+                        f = max(f, group_time(e[1], sl[0] + HON, r))
+                    if direct:
+                        f = max(f, group_time(direct, max(ISSUE, LANE * nl), r))
+                    key = (f, len(on) + len(rel), d)
+                    if best is None or key < best[0]:
+                        low = [e for sl, e in zip(slots, on) if sl[1] == 0]
+                        up = [e for sl, e in zip(slots, on) if sl[1] == 1]
+                        best = (key, direct, rel, low, up)
+    return best[1:]
+
+
+def make_calls(sender, ws, cores):
+    calls = []
+    for cl in by_width(ws):
+        off = [w for w in cl if cores[w[2]] // 8 != sender // 8]
+        on = [w for w in cl if cores[w[2]] // 8 == sender // 8]
+        while off or on:
+            call = []
+            for part, base in ((off[:8], 0), (on[:8], 8)):
+                if part:
+                    for m, w in zip(engine_masks(len(part), base), part):
+                        call.append((m, cores[w[2]], w[0], w[1], w[3]))
+            calls.append(call)
+            off, on = off[8:], on[8:]
+    return calls
+
+
+def build_plan(cores, route, cap, topo):
+    n = len(cores)
+    fill = [0] * n
+    writes = [[] for r in range(n)]
+    for r in range(n):
+        last = {}
+        for t in range(len(route[r])):
+            for e in route[r][t]:
+                if fill[e] < cap:
+                    w = last.get(e)
+                    if w is not None and w[0] + w[1] == t:
+                        w[1] += 1
+                    else:
+                        w = [t, 1, e, fill[e]]
+                        last[e] = w
+                        writes[r].append(w)
+                fill[e] += 1
+    plan = {"count": [min(f, cap) for f in fill], "arrive": [0] * n, "rank": {}, "helper": {}}
+    free = {}
+
+    def pool(base):
+        if base not in free:
+            free[base] = [base + k for k in range(8) if base + k not in cores]
+        return free[base]
+
+    def seat(pools, want):
+        for kinds in ((want,), (True, False)):
+            for p in pools:
+                for k in p:
+                    if topo.may_write(k, k ^ 8) in kinds and (topo.may_write(k, k ^ 8) or not want):
+                        p.remove(k)
+                        return k
+
+    chosen = []
+    for r in range(n):
+        a = cores[r]
+        A, B, S, C, D = [], [], [], [], []
+        for w in writes[r]:
+            b = cores[w[2]]
+            odd = (topo.chip(a) + topo.chip(b)) % 2 == 1
+            if b == a:
+                S.append(w)
+            elif topo.host(a) ^ topo.host(b) == 2:
+                (D if odd else C).append(w)
+            else:
+                (B if odd else A).append(w)
+        chosen.append(plan_source(r, A, B, S, C, D))
+    seats = {}
+    for stage in (1, 0):
+        for want in (True, False):
+            for r in range(n):
+                a = cores[r]
+                base = a - a % 8
+                direct, rel, low, up = chosen[r]
+                idle = [pool((base ^ 128) ^ 64)]
+                where = [pool(base)] if stage else ([pool(base ^ 384)] + idle if RELAY_ON_CABLED_CHIP else idle)
+                for name, groups in ((("low", low), ("up", up)) if stage else (("rel", rel),)):
+                    for i, e in enumerate(groups):
+                        if e[0] == want:
+                            seats[(r, name, i)] = seat(where, want)
+    for r in range(n):
+        a = cores[r]
+        direct, rel, low, up = chosen[r]
+        lanes = [[], []]
+        for name, lane, groups in (("rel", 0, rel), ("low", 0, low), ("up", 1, up)):
+            for i, e in enumerate(groups):
+                k = seats[(r, name, i)]
+                lanes[lane].append(k)
+                plan["helper"][k] = make_calls(k, e[1], cores)
+        plan["rank"][a] = (lanes, make_calls(a, direct, cores))
+    for calls in list(plan["helper"].values()) + [v[1] for v in plan["rank"].values()]:
+        for call in calls:
+            for m, d, t0, w, s0 in call:
+                plan["arrive"][cores.index(d)] += popcount(m)
+    return plan
+
+
+def send_tokens(g, core, T, topo, calls):
+    sent = 0
+    for call in calls:
+        trs = []
+        for m, d, t0, w, s0 in call:
+            rid, pid = topo.addr(d, core)
+            trs.append(bass.RemoteDMATransfer(dst_ids=[bass.DstId(rid=rid, pnc=pid)], dma_engine_mask=m,
+                                              remote_sem=T.sem.arrived, src=T.xs[:, t0:t0 + w], dst=T.land[:, s0:s0 + w]))
+            sent += popcount(m)
+        g.remote_dma_fused(trs, local_sem=T.sem.sent)
+    return sent
+
+
+def rank_program(g, core, T, topo):
+    if "p" not in PLAN:
+        PLAN["p"] = build_plan(list(T.cores), T.tables["ROUTE"], T.tables["CAP"], topo)
+    plan = PLAN["p"]
+    rank = T.rank_of(core)
+    if rank is None:
+        calls = plan["helper"].get(core)
+        if calls is None:
+            return
+        g.wait_ge(T.sem.xin, 8)
+        sent = send_tokens(g, core, T, topo, calls)
+        g.wait_ge(T.sem.sent, sent)
+        return
+    lanes, direct = plan["rank"][core]
+    g.dma_start(T.xs[:], T.x[:]).then_inc(T.sem.loaded, 16)
+    g.wait_ge(T.sem.loaded, 16)
+    sent = 0
+    trs = []
+    for lane, mask in ((0, 0x00FF), (1, 0xFF00)):
+        if lanes[lane]:
+            ids = []
+            for k in lanes[lane]:
+                rid, pid = topo.addr(k, core)
+                ids.append(bass.DstId(rid=rid, pnc=pid))
+            trs.append(bass.RemoteDMATransfer(dst_ids=ids, dma_engine_mask=mask, remote_sem=T.sem.xin,
+                                              srcs=[T.xs[:]], dsts=[T.xs[:] for k in lanes[lane]]))
+            sent += 8
+    if trs:
+        g.remote_dma_fused(trs, local_sem=T.sem.sent)
+    sent += send_tokens(g, core, T, topo, direct)
+    cnt = plan["count"][rank]
+    if cnt:
+        g.wait_ge(T.sem.arrived, plan["arrive"][rank])
+        g.dma_start(T.y[:, 0:cnt], T.land[:, 0:cnt]).then_inc(T.sem.stored, 16)
+    if sent:
+        g.wait_ge(T.sem.sent, sent)
+    if cnt:
+        g.wait_ge(T.sem.stored, 16)

@@ -6,11 +6,8 @@ SCRATCH = {
 }
 SEMAPHORES = ["loaded", "stored", "xin", "arrived", "sent"]
 
-ISSUE = 20
-HON = 40
-HOFF = 60
-ORDER = 0.5
-LANE = 16
+MACHINES = [(rho, issue, 0.5, 0.8, order) for rho, issue in ((0.005, 1.0), (0.02, 0.4), (0.06, 0.1)) for order in (0.0, 1.0)]
+BASE = 4.0
 RELAY_ON_CABLED_CHIP = True
 
 PLAN = {}
@@ -53,14 +50,13 @@ def by_width(ws):
     return [out[k] for k in sorted(out)]
 
 
-def group_time(ws, start, own):
+def group_time(ws, start, own, mc):
     end = start
     i = 0
     for cl in by_width(ws):
-        off = [w for w in cl if w[2] != own]
-        n = max(len(off), 1)
+        n = max(len([w for w in cl if w[2] != own]), 1)
         while n > 0:
-            end = max(end, start + i * ISSUE) + LANE * pow2ceil(min(n, 8))
+            end = max(end, start + i * mc[1]) + 16 * mc[0] * pow2ceil(min(n, 8))
             n -= 8
             i += 1
     return end
@@ -78,49 +74,61 @@ def pack(cross, plain, m):
     return gc, gp
 
 
-def arrival(p, n):
-    return LANE * (ORDER * (p + 1) + (1.0 - ORDER) * n)
+def singles(ws):
+    return [[w[0] + i, 1, w[2], w[3] + i] for w in ws for i in range(w[1])]
+
+
+def load(e):
+    return (-len(e[1]), -len(by_width(e[1])))
 
 
 def plan_source(r, A, B, S, C, D):
-    best = None
-    A = sorted(A, key=lambda w: (w[1], w[0]))
-    for md in (1, 2, 4, 8):
-        rc, rp = pack(D, C, md)
-        if len(rc) > 4 or len(rc) + len(rp) > 8:
-            continue
-        rel = [(True, g) for g in rc] + [(False, g) for g in rp]
-        rel.sort(key=lambda e: -group_time(e[1], 0, r))
-        for mo in (1, 2, 4, 8):
-            for d in range(len(A) + 1):
-                direct = A[:d]
-                gc, gp = pack(B, A[d:], mo)
-                if S and not gc and not gp:
-                    gp = [[]]
-                if len(gc) > 4 or len(gc) + len(gp) > 7:
+    cands = []
+    for split in (False, True):
+        if split:
+            A, B, C, D = singles(A), singles(B), singles(C), singles(D)
+        for rev in (1, -1):
+            A = sorted(A, key=lambda w: (rev * w[1], w[0]))
+            for md in (1, 2, 4, 8):
+                rc, rp = pack(D, C, md)
+                if len(rc) > 4 or len(rc) + len(rp) > 8:
                     continue
-                on = [(True, g) for g in gc] + [(False, g) for g in gp]
-                on.sort(key=lambda e: -group_time(e[1], 0, r))
-                if S:
-                    on[-1] = (on[-1][0], on[-1][1] + S)
-                for nlow in range(len(on) + 1):
-                    nl, nu = len(rel) + nlow, len(on) - nlow
-                    slots = [(arrival(p, nu), 1, p) for p in range(nu)]
-                    slots += [(arrival(p, nl), 0, p) for p in range(len(rel), nl)]
-                    slots.sort()
-                    f = 0
-                    for p, e in enumerate(rel):
-                        f = max(f, group_time(e[1], arrival(p, nl) + HOFF, r))
-                    for sl, e in zip(slots, on):
-                        f = max(f, group_time(e[1], sl[0] + HON, r))
-                    if direct:
-                        f = max(f, group_time(direct, max(ISSUE, LANE * nl), r))
-                    key = (f, len(on) + len(rel), d)
-                    if best is None or key < best[0]:
-                        low = [e for sl, e in zip(slots, on) if sl[1] == 0]
-                        up = [e for sl, e in zip(slots, on) if sl[1] == 1]
-                        best = (key, direct, rel, low, up)
-    return best[1:]
+                rel = sorted([(True, g) for g in rc] + [(False, g) for g in rp], key=load)
+                for mo in (1, 2, 4, 8):
+                    for d in range(len(A) + 1):
+                        direct = A[:d]
+                        gc, gp = pack(B, A[d:], mo)
+                        if S and not gc and not gp:
+                            gp = [[]]
+                        if len(gc) > 4 or len(gc) + len(gp) > 7:
+                            continue
+                        on = sorted([(True, g) for g in gc] + [(False, g) for g in gp], key=load)
+                        if S:
+                            on[-1] = (on[-1][0], on[-1][1] + S)
+                        for nlow in range(len(on) + 1):
+                            nl, nu = len(rel) + nlow, len(on) - nlow
+                            slots = sorted([(p, 1) for p in range(nu)] + [(p, 0) for p in range(len(rel), nl)])
+                            fs = []
+                            for mc in MACHINES:
+                                f = 0
+                                for (p, lane), e, hop in ([((p, 0), e, mc[3]) for p, e in enumerate(rel)]
+                                                          + [(sl, e, mc[2]) for sl, e in zip(slots, on)]):
+                                    n = nu if lane else nl
+                                    at = 16 * mc[0] * (p + 1 if mc[4] else n)
+                                    f = max(f, group_time(e[1], at + hop + mc[1], r, mc))
+                                if direct:
+                                    f = max(f, group_time(direct, max(mc[1], 16 * mc[0] * nl), r, mc))
+                                fs.append(f)
+                            low = [e for sl, e in zip(slots, on) if sl[1] == 0]
+                            up = [e for sl, e in zip(slots, on) if sl[1] == 1]
+                            cands.append((fs, len(on) + len(rel), d, (direct, rel, low, up)))
+    least = [min(c[0][i] for c in cands) for i in range(len(MACHINES))]
+    best = None
+    for fs, k, d, what in cands:
+        key = (round(max((BASE + f) / (BASE + m) for f, m in zip(fs, least)), 4), k, d)
+        if best is None or key < best[0]:
+            best = (key, what)
+    return best[1]
 
 
 def make_calls(sender, ws, cores):

@@ -8,7 +8,7 @@ SEMAPHORES = ["loaded", "stored", "xin", "arrived", "sent"]
 
 MACHINES = [(rho, issue, 0.5, 0.8, order) for rho, issue in ((0.005, 1.0), (0.02, 0.4), (0.06, 0.1)) for order in (0.0, 1.0)]
 BASE = 4.0
-RELAY_ON_CABLED_CHIP = True
+RELAY_ON_CABLED_CHIP = False
 
 PLAN = {}
 

@@ -8,7 +8,6 @@ SEMAPHORES = ["loaded", "stored", "xin", "arrived", "sent"]
 
 MACHINES = [(rho, issue, 0.5, 0.8, order) for rho, issue in ((0.005, 1.0), (0.02, 0.4), (0.06, 0.1)) for order in (0.0, 1.0)]
 BASE = 4.0
-RELAY_ON_CABLED_CHIP = False
 
 PLAN = {}
 
@@ -172,13 +171,12 @@ def build_plan(cores, route, cap, topo):
             free[base] = [base + k for k in range(8) if base + k not in cores]
         return free[base]
 
-    def seat(pools, want):
+    def seat(p, want):
         for kinds in ((want,), (True, False)):
-            for p in pools:
-                for k in p:
-                    if topo.may_write(k, k ^ 8) in kinds and (topo.may_write(k, k ^ 8) or not want):
-                        p.remove(k)
-                        return k
+            for k in p:
+                if topo.may_write(k, k ^ 8) in kinds and (topo.may_write(k, k ^ 8) or not want):
+                    p.remove(k)
+                    return k
 
     chosen = []
     for r in range(n):
@@ -195,18 +193,14 @@ def build_plan(cores, route, cap, topo):
                 (B if odd else A).append(w)
         chosen.append(plan_source(r, A, B, S, C, D))
     seats = {}
-    for stage in (1, 0):
-        for want in (True, False):
-            for r in range(n):
-                a = cores[r]
-                base = a - a % 8
-                direct, rel, low, up = chosen[r]
-                idle = [pool((base ^ 128) ^ 64)]
-                where = [pool(base)] if stage else ([pool(base ^ 384)] + idle if RELAY_ON_CABLED_CHIP else idle)
-                for name, groups in ((("low", low), ("up", up)) if stage else (("rel", rel),)):
-                    for i, e in enumerate(groups):
-                        if e[0] == want:
-                            seats[(r, name, i)] = seat(where, want)
+    for want in (True, False):
+        for r in range(n):
+            base = cores[r] - cores[r] % 8
+            direct, rel, low, up = chosen[r]
+            for name, groups, where in (("low", low, base), ("up", up, base), ("rel", rel, (base ^ 128) ^ 64)):
+                for i, e in enumerate(groups):
+                    if e[0] == want:
+                        seats[(r, name, i)] = seat(pool(where), want)
     for r in range(n):
         a = cores[r]
         direct, rel, low, up = chosen[r]

import concourse.bass as bass

SCRATCH = {
    "xs": ("sbuf", [128, 16], "float32"),
    "land": ("sbuf", [128, 12], "float32"),
}
SEMAPHORES = ["loaded", "stored", "xin", "arrived", "sent"]

MACHINES = [(rho, issue, 0.5, 0.8, order) for rho, issue in ((0.005, 1.0), (0.02, 0.4), (0.06, 0.1)) for order in (0.0, 1.0)]
BASE = 4.0

PLAN = {}


def pow2ceil(n):
    p = 1
    while p < n:
        p *= 2
    return p


def popcount(m):
    n = 0
    while m:
        n += m & 1
        m >>= 1
    return n


def engine_masks(n, base):
    each = 8 // pow2ceil(n)
    sizes = [each] * n
    spare = 8 - each * n
    for i in range(n):
        if spare >= each:
            sizes[i] += each
            spare -= each
    masks, at = [], base
    for s in sizes:
        masks.append(((1 << s) - 1) << at)
        at += s
    return masks


def by_width(ws):
    out = {}
    for w in ws:
        out.setdefault(w[1], []).append(w)
    return [out[k] for k in sorted(out)]


def group_time(ws, start, own, mc):
    end = start
    i = 0
    for cl in by_width(ws):
        n = max(len([w for w in cl if w[2] != own]), 1)
        while n > 0:
            end = max(end, start + i * mc[1]) + 16 * mc[0] * pow2ceil(min(n, 8))
            n -= 8
            i += 1
    return end


def chunks(ws, m):
    ws = sorted(ws, key=lambda w: (w[1], w[0]))
    return [ws[i:i + m] for i in range(0, len(ws), m)]


def pack(cross, plain, m):
    gc, gp = chunks(cross, m), chunks(plain, m)
    if gc and gp and len(gc[-1]) + len(gp[-1]) <= m:
        gc[-1] = gc[-1] + gp.pop()
    return gc, gp


def singles(ws):
    return [[w[0] + i, 1, w[2], w[3] + i] for w in ws for i in range(w[1])]


def load(e):
    return (-len(e[1]), -len(by_width(e[1])))


def plan_source(r, A, B, S, C, D):
    cands = []
    for split in (False, True):
        if split:
            A, B, C, D = singles(A), singles(B), singles(C), singles(D)
        for rev in (1, -1):
            A = sorted(A, key=lambda w: (rev * w[1], w[0]))
            for md in (1, 2, 4, 8):
                rc, rp = pack(D, C, md)
                if len(rc) > 4 or len(rc) + len(rp) > 8:
                    continue
                rel = sorted([(True, g) for g in rc] + [(False, g) for g in rp], key=load)
                for mo in (1, 2, 4, 8):
                    for d in range(len(A) + 1):
                        direct = A[:d]
                        gc, gp = pack(B, A[d:], mo)
                        if S and not gc and not gp:
                            gp = [[]]
                        if len(gc) > 4 or len(gc) + len(gp) > 7:
                            continue
                        on = sorted([(True, g) for g in gc] + [(False, g) for g in gp], key=load)
                        if S:
                            on[-1] = (on[-1][0], on[-1][1] + S)
                        for nlow in range(len(on) + 1):
                            nl, nu = len(rel) + nlow, len(on) - nlow
                            slots = sorted([(p, 1) for p in range(nu)] + [(p, 0) for p in range(len(rel), nl)])
                            fs = []
                            for mc in MACHINES:
                                f = 0
                                for (p, lane), e, hop in ([((p, 0), e, mc[3]) for p, e in enumerate(rel)]
                                                          + [(sl, e, mc[2]) for sl, e in zip(slots, on)]):
                                    n = nu if lane else nl
                                    at = 16 * mc[0] * (p + 1 if mc[4] else n)
                                    f = max(f, group_time(e[1], at + hop + mc[1], r, mc))
                                if direct:
                                    f = max(f, group_time(direct, max(mc[1], 16 * mc[0] * nl), r, mc))
                                fs.append(f)
                            low = [e for sl, e in zip(slots, on) if sl[1] == 0]
                            up = [e for sl, e in zip(slots, on) if sl[1] == 1]
                            cands.append((fs, len(on) + len(rel), d, (direct, rel, low, up)))
    least = [min(c[0][i] for c in cands) for i in range(len(MACHINES))]
    best = None
    for fs, k, d, what in cands:
        key = (round(max((BASE + f) / (BASE + m) for f, m in zip(fs, least)), 4), k, d)
        if best is None or key < best[0]:
            best = (key, what)
    return best[1]


def make_calls(sender, ws, cores):
    calls = []
    for cl in by_width(ws):
        off = [w for w in cl if cores[w[2]] // 8 != sender // 8]
        on = [w for w in cl if cores[w[2]] // 8 == sender // 8]
        while off or on:
            call = []
            for part, base in ((off[:8], 0), (on[:8], 8)):
                if part:
                    for m, w in zip(engine_masks(len(part), base), part):
                        call.append((m, cores[w[2]], w[0], w[1], w[3]))
            calls.append(call)
            off, on = off[8:], on[8:]
    return calls


def build_plan(cores, route, cap, topo):
    n = len(cores)
    fill = [0] * n
    writes = [[] for r in range(n)]
    for r in range(n):
        last = {}
        for t in range(len(route[r])):
            for e in route[r][t]:
                if fill[e] < cap:
                    w = last.get(e)
                    if w is not None and w[0] + w[1] == t:
                        w[1] += 1
                    else:
                        w = [t, 1, e, fill[e]]
                        last[e] = w
                        writes[r].append(w)
                fill[e] += 1
    plan = {"count": [min(f, cap) for f in fill], "arrive": [0] * n, "rank": {}, "helper": {}}
    free = {}

    def pool(base):
        if base not in free:
            free[base] = [base + k for k in range(8) if base + k not in cores]
        return free[base]

    def seat(p, want):
        for kinds in ((want,), (True, False)):
            for k in p:
                if topo.may_write(k, k ^ 8) in kinds and (topo.may_write(k, k ^ 8) or not want):
                    p.remove(k)
                    return k

    chosen = []
    for r in range(n):
        a = cores[r]
        A, B, S, C, D = [], [], [], [], []
        for w in writes[r]:
            b = cores[w[2]]
            odd = (topo.chip(a) + topo.chip(b)) % 2 == 1
            if b == a:
                S.append(w)
            elif topo.host(a) ^ topo.host(b) == 2:
                (D if odd else C).append(w)
            else:
                (B if odd else A).append(w)
        chosen.append(plan_source(r, A, B, S, C, D))
    seats = {}
    for want in (True, False):
        for r in range(n):
            base = cores[r] - cores[r] % 8
            direct, rel, low, up = chosen[r]
            for name, groups, where in (("low", low, base), ("up", up, base), ("rel", rel, (base ^ 128) ^ 64)):
                for i, e in enumerate(groups):
                    if e[0] == want:
                        seats[(r, name, i)] = seat(pool(where), want)
    for r in range(n):
        a = cores[r]
        direct, rel, low, up = chosen[r]
        lanes = [[], []]
        for name, lane, groups in (("rel", 0, rel), ("low", 0, low), ("up", 1, up)):
            for i, e in enumerate(groups):
                k = seats[(r, name, i)]
                lanes[lane].append(k)
                plan["helper"][k] = make_calls(k, e[1], cores)
        plan["rank"][a] = (lanes, make_calls(a, direct, cores))
    for calls in list(plan["helper"].values()) + [v[1] for v in plan["rank"].values()]:
        for call in calls:
            for m, d, t0, w, s0 in call:
                plan["arrive"][cores.index(d)] += popcount(m)
    return plan


def send_tokens(g, core, T, topo, calls):
    sent = 0
    for call in calls:
        trs = []
        for m, d, t0, w, s0 in call:
            rid, pid = topo.addr(d, core)
            trs.append(bass.RemoteDMATransfer(dst_ids=[bass.DstId(rid=rid, pnc=pid)], dma_engine_mask=m,
                                              remote_sem=T.sem.arrived, src=T.xs[:, t0:t0 + w], dst=T.land[:, s0:s0 + w]))
            sent += popcount(m)
        g.remote_dma_fused(trs, local_sem=T.sem.sent)
    return sent


def rank_program(g, core, T, topo):
    if "p" not in PLAN:
        PLAN["p"] = build_plan(list(T.cores), T.tables["ROUTE"], T.tables["CAP"], topo)
    plan = PLAN["p"]
    rank = T.rank_of(core)
    if rank is None:
        calls = plan["helper"].get(core)
        if calls is None:
            return
        g.wait_ge(T.sem.xin, 8)
        sent = send_tokens(g, core, T, topo, calls)
        g.wait_ge(T.sem.sent, sent)
        return
    lanes, direct = plan["rank"][core]
    g.dma_start(T.xs[:], T.x[:]).then_inc(T.sem.loaded, 16)
    g.wait_ge(T.sem.loaded, 16)
    sent = 0
    trs = []
    for lane, mask in ((0, 0x00FF), (1, 0xFF00)):
        if lanes[lane]:
            ids = []
            for k in lanes[lane]:
                rid, pid = topo.addr(k, core)
                ids.append(bass.DstId(rid=rid, pnc=pid))
            trs.append(bass.RemoteDMATransfer(dst_ids=ids, dma_engine_mask=mask, remote_sem=T.sem.xin,
                                              srcs=[T.xs[:]], dsts=[T.xs[:] for k in lanes[lane]]))
            sent += 8
    if trs:
        g.remote_dma_fused(trs, local_sem=T.sem.sent)
    sent += send_tokens(g, core, T, topo, direct)
    cnt = plan["count"][rank]
    if cnt:
        g.wait_ge(T.sem.arrived, plan["arrive"][rank])
        g.dma_start(T.y[:, 0:cnt], T.land[:, 0:cnt]).then_inc(T.sem.stored, 16)
    if sent:
        g.wait_ge(T.sem.sent, sent)
    if cnt:
        g.wait_ge(T.sem.stored, 16)
